import numpy as np
import ml_dtypes


def mxq(x, axis, fmt="e4m3"):
    dtype, down = {"e4m3": (ml_dtypes.float8_e4m3fn, 7), "e5m2": (ml_dtypes.float8_e5m2, 14)}[fmt]
    v = np.moveaxis(np.asarray(x, np.float32).astype(ml_dtypes.bfloat16).astype(np.float64), axis, -1)
    blocks = v.reshape(v.shape[:-1] + (-1, 32))
    amax = np.abs(blocks).max(-1, keepdims=True)
    byte = np.maximum(np.where(amax > 0, np.frexp(amax)[1] - 1 + 127, 0) - down, 1)
    scale = np.exp2(byte - 127.0)
    codes = (blocks / scale).astype(np.float32).astype(dtype).astype(np.float64)
    return np.moveaxis((codes * scale).reshape(v.shape), -1, axis)


WIDE = False


def mx_kscale(k):
    if not WIDE:
        return np.ones(k)
    levels = np.array([30, -30])
    if k % 512:
        return np.exp2(np.random.permutation(np.resize(levels, k // 32))).repeat(32)
    a = np.empty((k // 512, 16))
    for p in range(k // 512):
        a[p, :8] = np.random.permutation(np.resize(levels, 8))
        for g in range(8):
            far = levels[np.abs(levels - a[p, g]) >= 10]
            a[p, g + 8] = far[np.random.randint(len(far))]
    return np.exp2(a.ravel()).repeat(32)


def f64(x):
    return np.asarray(x).astype(np.float64)


def striped(idx):
    return np.tile(np.asarray(idx).reshape(-1, 16).T, (8, 1)).astype(np.uint16)


def unstriped(offs):
    return offs[:16].T.reshape(-1).astype(np.int64)


E2M1 = np.array([0.0, 0.5, 1.0, 1.5, 2.0, 3.0, 4.0, 6.0, -0.0, -0.5, -1.0, -1.5, -2.0, -3.0, -4.0, -6.0])


def pack_weight(w, fmt):
    k, n = w.shape
    w = f64(np.asarray(w, np.float32).astype(ml_dtypes.bfloat16)).reshape(k // 32, 32, n)
    amax = np.abs(w).max(1)
    if fmt in ("e4m3", "e5m2"):
        byte = np.frexp(amax)[1] - 1 + 127 - (7 if fmt == "e4m3" else 14)
    else:
        mant, ex = np.frexp(amax / 6.0)
        byte = np.where(mant > 0.5, ex, ex - 1) + 127
    byte = np.clip(np.where(amax > 0, byte, 1), 1, 254)
    scaled = (w * np.exp2(127.0 - byte)[:, None, :]).reshape(k, n).astype(np.float32)
    by_word = np.ascontiguousarray(scaled.reshape(k // 512, 128, 4, n).transpose(0, 1, 3, 2))
    if fmt in ("e4m3", "e5m2"):
        words = by_word.astype(ml_dtypes.float8_e4m3fn if fmt == "e4m3" else ml_dtypes.float8_e5m2).view(np.uint8)
    else:
        c = by_word.astype(ml_dtypes.float4_e2m1fn).view(np.uint8) & 0xF
        words = (c[..., 0::2] | (c[..., 1::2] << 4)).reshape(k // 512, 128, 2 * n)
    return np.ascontiguousarray(words), np.ascontiguousarray(byte.astype(np.uint8).reshape(k // 512, 16, n))


def unpack_weight(words, scales, fmt):
    g, _, n = scales.shape
    words = np.ascontiguousarray(words).reshape(g, 128, n, -1)
    if fmt in ("e4m3", "e5m2"):
        vals = words.view(ml_dtypes.float8_e4m3fn if fmt == "e4m3" else ml_dtypes.float8_e5m2).astype(np.float64)
    else:
        nib = np.empty((g, 128, n, 4), np.uint8)
        nib[..., 0::2] = words & 0xF
        nib[..., 1::2] = words >> 4
        vals = E2M1[nib]
    vals = vals * np.repeat(np.exp2(scales.astype(np.float64) - 127.0), 8, axis=1)[..., None]
    return vals.transpose(0, 1, 3, 2).reshape(g * 512, n)


K, T, J, R, O, N = 512, 2048, 256, 512, 128, 256


def setup_inputs():
    n = np.random.standard_normal
    idx = np.random.permutation(T)[:J]
    idx2 = np.random.permutation(T)[:J]
    idx3 = np.random.permutation(T)[:J]
    idx4 = np.random.permutation(J)[:O]
    idx5 = np.random.permutation(J)[:O]
    fk = mx_kscale(K)
    fr = mx_kscale(R)
    xtp = pack_weight(n((K, T)) / fk[:, None], "e2m1")
    wp = pack_weight(n((K, R)) * 1 / np.sqrt(K) * fk[:, None] * fr, "e5m2")
    wbp = pack_weight(n((R, N)) * 1 / np.sqrt(R) / fr[:, None], "e4m3")
    return {
        "xt_words": xtp[0],
        "xt_scales": xtp[1],
        "w_words": wp[0],
        "w_scales": wp[1],
        "wb_words": wbp[0],
        "wb_scales": wbp[1],
        "offs": striped(idx),
        "offs2": striped(idx2),
        "offs3": striped(idx3),
        "offs4": striped(idx4),
        "offs5": striped(idx5),
    }


def reference(xt_words, xt_scales, w_words, w_scales, wb_words, wb_scales, offs, offs2, offs3, offs4, offs5):
    idx = unstriped(offs)
    idx2 = unstriped(offs2)
    idx3 = unstriped(offs3)
    idx4 = unstriped(offs4)
    idx5 = unstriped(offs5)
    xtu = unpack_weight(xt_words, xt_scales, "e2m1")
    wu = unpack_weight(w_words, w_scales, "e5m2")
    wbu = unpack_weight(wb_words, wb_scales, "e4m3")
    xtidxg = xtu[:, idx]
    a = wu.T @ xtidxg
    xtidx2g = xtu[:, idx2]
    b = wu.T @ xtidx2g
    xtidx3g = xtu[:, idx3]
    g0 = wu.T @ xtidx3g
    c1 = np.maximum(b, g0)
    hid = np.abs(a[:, idx4] - c1[:, idx5])
    hidq = mxq(hid, 0, "e5m2")
    y = wbu.T @ hidq
    return y

@@ -1,0 +1,173 @@
+from contextlib import ExitStack
+
+import concourse.mybir as mybir
+
+K, T, J, R, O, N = 512, 2048, 256, 512, 128, 256
+FLOPS = 2 * K * R * 3 * J + 2 * R * N * O
+
+F32 = mybir.dt.float32
+BF16 = mybir.dt.bfloat16
+I32 = mybir.dt.int32
+U32 = mybir.dt.uint32
+U16 = mybir.dt.uint16
+U8 = mybir.dt.uint8
+E2M1X4 = mybir.dt.float4_e2m1fn_x4
+E5M2X4 = mybir.dt.float8_e5m2_x4
+E4M3X4 = mybir.dt.float8_e4m3fn_x4
+ALU = mybir.AluOpType
+ACT = mybir.ActivationFunctionType
+
+P = 128
+PACK = 4
+QUADS = 4
+PAIRS = 2
+
+
+def load_scale_rows(nc, plane, rows):
+    for q in range(QUADS):
+        nc.sync.dma_start(out=plane[32 * q : 32 * q + 4, :].bitcast(I32), in_=rows[4 * q : 4 * q + 4, :].bitcast(I32))
+
+
+def tile_list_triple_looked_one_plain_kernel(
+    tc, xt_words, xt_scales, w_words, w_scales, wb_words, wb_scales, offs, offs2, offs3, offs4, offs5, out
+):
+    nc = tc.nc
+    with ExitStack() as ctx:
+        lists = ctx.enter_context(tc.tile_pool(name="lists", bufs=1))
+        keep = ctx.enter_context(tc.tile_pool(name="keep", bufs=1))
+        psum = ctx.enter_context(tc.psum_pool(name="psum", bufs=1))
+
+        list_a = lists.tile([P, J // 16], U16, name="list_a")
+        list_b = lists.tile([P, J // 16], U16, name="list_b")
+        list_g = lists.tile([P, J // 16], U16, name="list_g")
+        pick_a = lists.tile([P, O // 16], U16, name="pick_a")
+        pick_c = lists.tile([P, O // 16], U16, name="pick_c")
+
+        x_codes = keep.tile([P, T], U16, name="x_codes", align_bytes=64)
+        x_plane = keep.tile([P, T], U8, name="x_plane", align_bytes=64)
+        w_raw = keep.tile([P, R], U32, name="w_raw", align_bytes=64)
+        w_plane_raw = keep.tile([P, R], U8, name="w_plane_raw", align_bytes=64)
+        wb_codes = keep.tile([P, N], U32, name="wb_codes", align_bytes=64)
+        wb_plane = keep.tile([P, N], U8, name="wb_plane", align_bytes=64)
+
+        w_scale_rows = keep.tile([4, QUADS, R], U8, name="w_scale_rows", align_bytes=64)
+
+        nc.vector.memset(x_plane[:].bitcast(I32), 0)
+        nc.vector.memset(w_plane_raw[:].bitcast(I32), 0)
+        nc.vector.memset(wb_plane[:].bitcast(I32), 0)
+
+        nc.scalar.dma_start(
+            out=w_scale_rows[:].bitcast(I32), in_=w_scales[0].bitcast(I32).rearrange("(q r) c -> r q c", r=4)
+        )
+        nc.sync.dma_start(list_a[:], offs)
+        nc.sync.dma_start(out=x_codes[:].bitcast(I32), in_=xt_words[0].bitcast(I32))
+        load_scale_rows(nc, x_plane, xt_scales[0])
+        nc.sync.dma_start(out=w_raw[:].bitcast(I32), in_=w_words[0].rearrange("p n t -> p (n t)").bitcast(I32))
+        nc.sync.dma_start(list_b[:], offs2)
+        nc.sync.dma_start(list_g[:], offs3)
+        nc.sync.dma_start(pick_a[:], offs4)
+        nc.sync.dma_start(pick_c[:], offs5)
+        nc.sync.dma_start(out=wb_codes[:].bitcast(I32), in_=wb_words[0].rearrange("p n t -> p (n t)").bitcast(I32))
+        load_scale_rows(nc, wb_plane, wb_scales[0])
+
+        for q in range(QUADS):
+            nc.vector.tensor_copy(
+                out=w_plane_raw[32 * q : 32 * q + 4, :].bitcast(I32), in_=w_scale_rows[:, q, :].bitcast(I32)
+            )
+
+        w_codes = [keep.tile([P, 2, P], U32, name="w_codes%d" % h, align_bytes=64) for h in range(PAIRS)]
+        w_plane = keep.tile([P, PACK, P], U8, name="w_plane", align_bytes=64)
+
+        def look_up_tokens(offsets, name):
+            codes = keep.tile([P, J], U16, name=name + "_codes", align_bytes=64)
+            plane = keep.tile([P, J], U8, name=name + "_plane", align_bytes=64)
+            nc.vector.tensor_copy(out=codes[:], in_=x_codes[:].indirect(offsets[:]))
+            nc.vector.tensor_copy(out=plane[:], in_=x_plane[:].indirect(offsets[:]))
+            return codes, plane
+
+        def first_product(codes, plane, name, per_bank):
+            banks = [
+                psum.tile([P, per_bank, J], F32, name="%s_bank%d" % (name, h), tag="%s_bank%d" % (name, h)) for h in range(PACK // per_bank)
+            ]
+            sums = [banks[t // per_bank][:, t % per_bank, :] for t in range(PACK)]
+            for t in range(PACK):
+                nc.tensor.matmul_mx(
+                    out=sums[t],
+                    lhsT=w_codes[t // 2][:, t % 2, :].bitcast(E5M2X4),
+                    lhsT_scale=w_plane[:, t, :],
+                    rhs=codes[:].bitcast(E2M1X4),
+                    rhs_scale=plane[:],
+                    start=True,
+                    stop=True,
+                )
+            return banks, sums
+
+        nc.vector.tensor_copy(
+            out=w_plane[:].rearrange("p t m -> p m t"), in_=w_plane_raw[:].rearrange("p (m t) -> p m t", t=PACK)
+        )
+        tokens_a = look_up_tokens(list_a, "xa")
+        for h in range(PAIRS):
+            nc.scalar.copy(
+                out=w_codes[h][:].rearrange("p t m -> p m t"),
+                in_=w_raw[:].rearrange("p (m t) -> p m t", t=PACK)[:, :, 2 * h : 2 * h + 2],
+            )
+        a_banks, a_sums = first_product(*tokens_a, "a", 2)
+        b_banks, b_sums = first_product(*look_up_tokens(list_b, "xb"), "b", 2)
+        g_banks, g_sums = first_product(*look_up_tokens(list_g, "xg"), "g", 1)
+
+        a_rows = [keep.tile([P, J], F32, name="a_rows%d" % t) for t in range(PACK)]
+        c_rows = [keep.tile([P, J], F32, name="c_rows%d" % t) for t in range(PACK)]
+        b_rows = keep.tile([P, PACK, J], F32, name="b_rows")
+        a_picked = keep.tile([P, PACK, O], F32, name="a_picked")
+        diff = keep.tile([P, PACK, O], F32, name="diff")
+
+        for t in range(PACK):
+            nc.scalar.activation(out=a_rows[t][:], in_=a_sums[t], func=ACT.Copy)
+        for h in range(PAIRS):
+            nc.scalar.activation(out=b_rows[:, 2 * h : 2 * h + 2, :], in_=b_banks[h][:], func=ACT.Copy)
+        for t in range(PACK):
+            nc.scalar.activation(out=a_picked[:, t, :], in_=a_rows[t][:].indirect(pick_a[:]), func=ACT.Copy)
+        for t in range(PACK):
+            nc.vector.tensor_tensor(out=c_rows[t][:], in0=g_sums[t], in1=b_rows[:, t, :], op=ALU.max)
+        for t in range(PACK):
+            nc.vector.tensor_tensor(
+                out=diff[:, t, :], in0=c_rows[t][:].indirect(pick_c[:]), in1=a_picked[:, t, :], op=ALU.subtract
+            )
+
+        hid = keep.tile([P, O, PACK], BF16, name="hid", align_bytes=64)
+        half = O // 2
+        diff_by_place = diff[:].rearrange("p t o -> p o t")
+        nc.scalar.activation(out=hid[:, half:, :], in_=diff_by_place[:, half:, :], func=ACT.Abs)
+        nc.vector.scalar_tensor_tensor(
+            out=hid[:, :half, :],
+            in0=diff_by_place[:, :half, :],
+            scalar=-1.0,
+            in1=diff_by_place[:, :half, :],
+            op0=ALU.mult,
+            op1=ALU.max,
+        )
+        hid_codes = keep.tile([P, O], U32, name="hid_codes", align_bytes=64)
+        hid_plane = keep.tile([P, O], U8, name="hid_plane", align_bytes=64)
+        nc.vector.quantize_mx(
+            out=hid_codes[:].bitcast(E5M2X4), scales=hid_plane[:], in_=hid[:].rearrange("p o t -> p (o t)")
+        )
+
+        for h in range(N // P):
+            cols = slice(h * P, (h + 1) * P)
+            y_bank = psum.tile([P, O], F32, name="y_bank%d" % h, tag="a_bank%d" % h)
+            nc.tensor.matmul_mx(
+                out=y_bank[:],
+                lhsT=wb_codes[:, cols].bitcast(E4M3X4),
+                lhsT_scale=wb_plane[:, cols],
+                rhs=hid_codes[:].bitcast(E5M2X4),
+                rhs_scale=hid_plane[:],
+                start=True,
+                stop=True,
+            )
+            y_rows = keep.tile([P, O], F32, name="y_rows%d" % h)
+            if h == 0:
+                nc.vector.tensor_copy(out=y_rows[:], in_=y_bank[:])
+                nc.sync.dma_start(out=out[cols, :], in_=y_rows[:])
+            else:
+                nc.scalar.copy(out=y_rows[:], in_=y_bank[:])
+                nc.scalar.dma_start(out=out[cols, :], in_=y_rows[:])

@@ -85,14 +85,11 @@ def tile_list_triple_looked_one_plain_kernel(
             nc.vector.tensor_copy(out=plane[:], in_=x_plane[:].indirect(offsets[:]))
             return codes, plane
 
-        def first_product(codes, plane, name, per_bank):
-            banks = [
-                psum.tile([P, per_bank, J], F32, name="%s_bank%d" % (name, h), tag="%s_bank%d" % (name, h)) for h in range(PACK // per_bank)
-            ]
-            sums = [banks[t // per_bank][:, t % per_bank, :] for t in range(PACK)]
+        def first_product(codes, plane, name, bank_set):
+            sums = [psum.tile([P, J], F32, name="%s_sum%d" % (name, t), tag="%s%d" % (bank_set, t)) for t in range(PACK)]
             for t in range(PACK):
                 nc.tensor.matmul_mx(
-                    out=sums[t],
+                    out=sums[t][:],
                     lhsT=w_codes[t // 2][:, t % 2, :].bitcast(E5M2X4),
                     lhsT_scale=w_plane[:, t, :],
                     rhs=codes[:].bitcast(E2M1X4),
@@ -100,10 +97,10 @@ def tile_list_triple_looked_one_plain_kernel(
                     start=True,
                     stop=True,
                 )
-            return banks, sums
+            return sums
 
         nc.vector.tensor_copy(
-            out=w_plane[:].rearrange("p t m -> p m t"), in_=w_plane_raw[:].rearrange("p (m t) -> p m t", t=PACK)
+            out=w_plane[:], in_=w_plane_raw[:].rearrange("p (m t) -> p t m", t=PACK)
         )
         tokens_a = look_up_tokens(list_a, "xa")
         for h in range(PAIRS):
@@ -111,38 +108,43 @@ def tile_list_triple_looked_one_plain_kernel(
                 out=w_codes[h][:].rearrange("p t m -> p m t"),
                 in_=w_raw[:].rearrange("p (m t) -> p m t", t=PACK)[:, :, 2 * h : 2 * h + 2],
             )
-        a_banks, a_sums = first_product(*tokens_a, "a", 2)
-        b_banks, b_sums = first_product(*look_up_tokens(list_b, "xb"), "b", 2)
-        g_banks, g_sums = first_product(*look_up_tokens(list_g, "xg"), "g", 1)
-
         a_rows = [keep.tile([P, J], F32, name="a_rows%d" % t) for t in range(PACK)]
         c_rows = [keep.tile([P, J], F32, name="c_rows%d" % t) for t in range(PACK)]
         b_rows = keep.tile([P, PACK, J], F32, name="b_rows")
         a_picked = keep.tile([P, PACK, O], F32, name="a_picked")
+        c_picked = keep.tile([P, 2, O], F32, name="c_picked")
         diff = keep.tile([P, PACK, O], F32, name="diff")
 
+        a_sums = first_product(*tokens_a, "a", "low")
         for t in range(PACK):
-            nc.scalar.activation(out=a_rows[t][:], in_=a_sums[t], func=ACT.Copy)
-        for h in range(PAIRS):
-            nc.scalar.activation(out=b_rows[:, 2 * h : 2 * h + 2, :], in_=b_banks[h][:], func=ACT.Copy)
+            nc.scalar.activation(out=a_rows[t][:], in_=a_sums[t][:], func=ACT.Copy)
+        b_sums = first_product(*look_up_tokens(list_b, "xb"), "b", "high")
         for t in range(PACK):
+            nc.scalar.activation(out=b_rows[:, t, :], in_=b_sums[t][:], func=ACT.Copy)
+        g_sums = first_product(*look_up_tokens(list_g, "xg"), "g", "low")
+        nc.vector.tensor_copy(out=a_picked[:, 0, :], in_=a_rows[0][:].indirect(pick_a[:]))
+        for t in (2, 3, 1):
             nc.scalar.activation(out=a_picked[:, t, :], in_=a_rows[t][:].indirect(pick_a[:]), func=ACT.Copy)
         for t in range(PACK):
-            nc.vector.tensor_tensor(out=c_rows[t][:], in0=g_sums[t], in1=b_rows[:, t, :], op=ALU.max)
-        for t in range(PACK):
+            nc.vector.tensor_tensor(out=c_rows[t][:], in0=g_sums[t][:], in1=b_rows[:, t, :], op=ALU.max)
+        for t in (0, 1):
+            nc.scalar.activation(out=c_picked[:, t, :], in_=c_rows[t][:].indirect(pick_c[:]), func=ACT.Copy)
+        for t in (2, 3):
             nc.vector.tensor_tensor(
                 out=diff[:, t, :], in0=c_rows[t][:].indirect(pick_c[:]), in1=a_picked[:, t, :], op=ALU.subtract
             )
+        nc.vector.tensor_tensor(out=diff[:, :2, :], in0=c_picked[:], in1=a_picked[:, :2, :], op=ALU.subtract)
 
         hid = keep.tile([P, O, PACK], BF16, name="hid", align_bytes=64)
         half = O // 2
         diff_by_place = diff[:].rearrange("p t o -> p o t")
-        nc.scalar.activation(out=hid[:, half:, :], in_=diff_by_place[:, half:, :], func=ACT.Abs)
+        nc.scalar.activation(out=hid[:, :, 2:], in_=diff_by_place[:, :, 2:], func=ACT.Abs)
+        nc.scalar.activation(out=hid[:, half:, :2], in_=diff_by_place[:, half:, :2], func=ACT.Abs)
         nc.vector.scalar_tensor_tensor(
-            out=hid[:, :half, :],
-            in0=diff_by_place[:, :half, :],
+            out=hid[:, :half, :2],
+            in0=diff_by_place[:, :half, :2],
             scalar=-1.0,
-            in1=diff_by_place[:, :half, :],
+            in1=diff_by_place[:, :half, :2],
             op0=ALU.mult,
             op1=ALU.max,
         )
@@ -154,7 +156,7 @@ def tile_list_triple_looked_one_plain_kernel(
 
         for h in range(N // P):
             cols = slice(h * P, (h + 1) * P)
-            y_bank = psum.tile([P, O], F32, name="y_bank%d" % h, tag="a_bank%d" % h)
+            y_bank = psum.tile([P, O], F32, name="y_bank%d" % h, tag="high%d" % h)
             nc.tensor.matmul_mx(
                 out=y_bank[:],
                 lhsT=wb_codes[:, cols].bitcast(E4M3X4),

from contextlib import ExitStack

import concourse.mybir as mybir

K, T, J, R, O, N = 512, 2048, 256, 512, 128, 256
FLOPS = 2 * K * R * 3 * J + 2 * R * N * O

F32 = mybir.dt.float32
BF16 = mybir.dt.bfloat16
I32 = mybir.dt.int32
U32 = mybir.dt.uint32
U16 = mybir.dt.uint16
U8 = mybir.dt.uint8
E2M1X4 = mybir.dt.float4_e2m1fn_x4
E5M2X4 = mybir.dt.float8_e5m2_x4
E4M3X4 = mybir.dt.float8_e4m3fn_x4
ALU = mybir.AluOpType
ACT = mybir.ActivationFunctionType

P = 128
PACK = 4
QUADS = 4
PAIRS = 2


def load_scale_rows(nc, plane, rows):
    for q in range(QUADS):
        nc.sync.dma_start(out=plane[32 * q : 32 * q + 4, :].bitcast(I32), in_=rows[4 * q : 4 * q + 4, :].bitcast(I32))


def tile_list_triple_looked_one_plain_kernel(
    tc, xt_words, xt_scales, w_words, w_scales, wb_words, wb_scales, offs, offs2, offs3, offs4, offs5, out
):
    nc = tc.nc
    with ExitStack() as ctx:
        lists = ctx.enter_context(tc.tile_pool(name="lists", bufs=1))
        keep = ctx.enter_context(tc.tile_pool(name="keep", bufs=1))
        psum = ctx.enter_context(tc.psum_pool(name="psum", bufs=1))

        list_a = lists.tile([P, J // 16], U16, name="list_a")
        list_b = lists.tile([P, J // 16], U16, name="list_b")
        list_g = lists.tile([P, J // 16], U16, name="list_g")
        pick_a = lists.tile([P, O // 16], U16, name="pick_a")
        pick_c = lists.tile([P, O // 16], U16, name="pick_c")

        x_codes = keep.tile([P, T], U16, name="x_codes", align_bytes=64)
        x_plane = keep.tile([P, T], U8, name="x_plane", align_bytes=64)
        w_raw = keep.tile([P, R], U32, name="w_raw", align_bytes=64)
        w_plane_raw = keep.tile([P, R], U8, name="w_plane_raw", align_bytes=64)
        wb_codes = keep.tile([P, N], U32, name="wb_codes", align_bytes=64)
        wb_plane = keep.tile([P, N], U8, name="wb_plane", align_bytes=64)

        w_scale_rows = keep.tile([4, QUADS, R], U8, name="w_scale_rows", align_bytes=64)

        nc.vector.memset(x_plane[:].bitcast(I32), 0)
        nc.vector.memset(w_plane_raw[:].bitcast(I32), 0)
        nc.vector.memset(wb_plane[:].bitcast(I32), 0)

        nc.scalar.dma_start(
            out=w_scale_rows[:].bitcast(I32), in_=w_scales[0].bitcast(I32).rearrange("(q r) c -> r q c", r=4)
        )
        nc.sync.dma_start(list_a[:], offs)
        nc.sync.dma_start(out=x_codes[:].bitcast(I32), in_=xt_words[0].bitcast(I32))
        load_scale_rows(nc, x_plane, xt_scales[0])
        nc.sync.dma_start(out=w_raw[:].bitcast(I32), in_=w_words[0].rearrange("p n t -> p (n t)").bitcast(I32))
        nc.sync.dma_start(list_b[:], offs2)
        nc.sync.dma_start(list_g[:], offs3)
        nc.sync.dma_start(pick_a[:], offs4)
        nc.sync.dma_start(pick_c[:], offs5)
        nc.sync.dma_start(out=wb_codes[:].bitcast(I32), in_=wb_words[0].rearrange("p n t -> p (n t)").bitcast(I32))
        load_scale_rows(nc, wb_plane, wb_scales[0])

        for q in range(QUADS):
            nc.vector.tensor_copy(
                out=w_plane_raw[32 * q : 32 * q + 4, :].bitcast(I32), in_=w_scale_rows[:, q, :].bitcast(I32)
            )

        w_codes = [keep.tile([P, 2, P], U32, name="w_codes%d" % h, align_bytes=64) for h in range(PAIRS)]
        w_plane = keep.tile([P, PACK, P], U8, name="w_plane", align_bytes=64)

        def look_up_tokens(offsets, name):
            codes = keep.tile([P, J], U16, name=name + "_codes", align_bytes=64)
            plane = keep.tile([P, J], U8, name=name + "_plane", align_bytes=64)
            nc.vector.tensor_copy(out=codes[:], in_=x_codes[:].indirect(offsets[:]))
            nc.vector.tensor_copy(out=plane[:], in_=x_plane[:].indirect(offsets[:]))
            return codes, plane

        def first_product(codes, plane, name, bank_set):
            sums = [psum.tile([P, J], F32, name="%s_sum%d" % (name, t), tag="%s%d" % (bank_set, t)) for t in range(PACK)]
            for t in range(PACK):
                nc.tensor.matmul_mx(
                    out=sums[t][:],
                    lhsT=w_codes[t // 2][:, t % 2, :].bitcast(E5M2X4),
                    lhsT_scale=w_plane[:, t, :],
                    rhs=codes[:].bitcast(E2M1X4),
                    rhs_scale=plane[:],
                    start=True,
                    stop=True,
                )
            return sums

        nc.vector.tensor_copy(
            out=w_plane[:], in_=w_plane_raw[:].rearrange("p (m t) -> p t m", t=PACK)
        )
        tokens_a = look_up_tokens(list_a, "xa")
        for h in range(PAIRS):
            nc.scalar.copy(
                out=w_codes[h][:].rearrange("p t m -> p m t"),
                in_=w_raw[:].rearrange("p (m t) -> p m t", t=PACK)[:, :, 2 * h : 2 * h + 2],
            )
        a_rows = [keep.tile([P, J], F32, name="a_rows%d" % t) for t in range(PACK)]
        c_rows = [keep.tile([P, J], F32, name="c_rows%d" % t) for t in range(PACK)]
        b_rows = keep.tile([P, PACK, J], F32, name="b_rows")
        a_picked = keep.tile([P, PACK, O], F32, name="a_picked")
        c_picked = keep.tile([P, 2, O], F32, name="c_picked")
        diff = keep.tile([P, PACK, O], F32, name="diff")

        a_sums = first_product(*tokens_a, "a", "low")
        for t in range(PACK):
            nc.scalar.activation(out=a_rows[t][:], in_=a_sums[t][:], func=ACT.Copy)
        b_sums = first_product(*look_up_tokens(list_b, "xb"), "b", "high")
        for t in range(PACK):
            nc.scalar.activation(out=b_rows[:, t, :], in_=b_sums[t][:], func=ACT.Copy)
        g_sums = first_product(*look_up_tokens(list_g, "xg"), "g", "low")
        nc.vector.tensor_copy(out=a_picked[:, 0, :], in_=a_rows[0][:].indirect(pick_a[:]))
        for t in (2, 3, 1):
            nc.scalar.activation(out=a_picked[:, t, :], in_=a_rows[t][:].indirect(pick_a[:]), func=ACT.Copy)
        for t in range(PACK):
            nc.vector.tensor_tensor(out=c_rows[t][:], in0=g_sums[t][:], in1=b_rows[:, t, :], op=ALU.max)
        for t in (0, 1):
            nc.scalar.activation(out=c_picked[:, t, :], in_=c_rows[t][:].indirect(pick_c[:]), func=ACT.Copy)
        for t in (2, 3):
            nc.vector.tensor_tensor(
                out=diff[:, t, :], in0=c_rows[t][:].indirect(pick_c[:]), in1=a_picked[:, t, :], op=ALU.subtract
            )
        nc.vector.tensor_tensor(out=diff[:, :2, :], in0=c_picked[:], in1=a_picked[:, :2, :], op=ALU.subtract)

        hid = keep.tile([P, O, PACK], BF16, name="hid", align_bytes=64)
        half = O // 2
        diff_by_place = diff[:].rearrange("p t o -> p o t")
        nc.scalar.activation(out=hid[:, :, 2:], in_=diff_by_place[:, :, 2:], func=ACT.Abs)
        nc.scalar.activation(out=hid[:, half:, :2], in_=diff_by_place[:, half:, :2], func=ACT.Abs)
        nc.vector.scalar_tensor_tensor(
            out=hid[:, :half, :2],
            in0=diff_by_place[:, :half, :2],
            scalar=-1.0,
            in1=diff_by_place[:, :half, :2],
            op0=ALU.mult,
            op1=ALU.max,
        )
        hid_codes = keep.tile([P, O], U32, name="hid_codes", align_bytes=64)
        hid_plane = keep.tile([P, O], U8, name="hid_plane", align_bytes=64)
        nc.vector.quantize_mx(
            out=hid_codes[:].bitcast(E5M2X4), scales=hid_plane[:], in_=hid[:].rearrange("p o t -> p (o t)")
        )

        for h in range(N // P):
            cols = slice(h * P, (h + 1) * P)
            y_bank = psum.tile([P, O], F32, name="y_bank%d" % h, tag="high%d" % h)
            nc.tensor.matmul_mx(
                out=y_bank[:],
                lhsT=wb_codes[:, cols].bitcast(E4M3X4),
                lhsT_scale=wb_plane[:, cols],
                rhs=hid_codes[:].bitcast(E5M2X4),
                rhs_scale=hid_plane[:],
                start=True,
                stop=True,
            )
            y_rows = keep.tile([P, O], F32, name="y_rows%d" % h)
            if h == 0:
                nc.vector.tensor_copy(out=y_rows[:], in_=y_bank[:])
                nc.sync.dma_start(out=out[cols, :], in_=y_rows[:])
            else:
                nc.scalar.copy(out=y_rows[:], in_=y_bank[:])
                nc.scalar.dma_start(out=out[cols, :], in_=y_rows[:])
